import numpy as np
import ml_dtypes


def mxq(x, axis, fmt="e4m3"):
    dtype, down = {"e4m3": (ml_dtypes.float8_e4m3fn, 7), "e5m2": (ml_dtypes.float8_e5m2, 14)}[fmt]
    v = np.moveaxis(np.asarray(x, np.float32).astype(ml_dtypes.bfloat16).astype(np.float64), axis, -1)
    blocks = v.reshape(v.shape[:-1] + (-1, 32))
    amax = np.abs(blocks).max(-1, keepdims=True)
    byte = np.maximum(np.where(amax > 0, np.frexp(amax)[1] - 1 + 127, 0) - down, 1)
    scale = np.exp2(byte - 127.0)
    codes = (blocks / scale).astype(np.float32).astype(dtype).astype(np.float64)
    return np.moveaxis((codes * scale).reshape(v.shape), -1, axis)


WIDE = False


def mx_kscale(k):
    if not WIDE:
        return np.ones(k)
    levels = np.array([10, -10, 5, -5, 0])
    if k % 512:
        return np.exp2(np.random.permutation(np.resize(levels, k // 32))).repeat(32)
    a = np.empty((k // 512, 16))
    for p in range(k // 512):
        a[p, :8] = np.random.permutation(np.resize(levels, 8))
        for g in range(8):
            far = levels[np.abs(levels - a[p, g]) >= 10]
            a[p, g + 8] = far[np.random.randint(len(far))]
    return np.exp2(a.ravel()).repeat(32)


def f64(x):
    return np.asarray(x).astype(np.float64)


def striped(idx):
    return np.tile(idx.reshape(-1, 16).T, (8, 1)).astype(np.uint16)


def unstriped(offs):
    return offs[:16].T.reshape(-1).astype(np.int64)


def pack_weight(w):
    k, n = w.shape
    w = f64(np.asarray(w, np.float32).astype(ml_dtypes.bfloat16)).reshape(k // 32, 32, n)
    amax = np.abs(w).max(1)
    byte = np.clip(np.where(amax > 0, np.frexp(amax)[1] - 1 + 127 - 7, 1), 1, 254)
    scaled = (w * np.exp2(127.0 - byte)[:, None, :]).reshape(k, n).astype(np.float32)
    words = np.ascontiguousarray(scaled.reshape(k // 512, 128, 4, n).transpose(0, 1, 3, 2)).astype(ml_dtypes.float8_e4m3fn).view(np.uint8)
    return words, np.ascontiguousarray(byte.astype(np.uint8).reshape(k // 512, 16, n))


def unpack_weight(words, scales):
    g, p, n, _ = words.shape
    vals = np.ascontiguousarray(words).view(ml_dtypes.float8_e4m3fn).astype(np.float64) * np.repeat(np.exp2(scales.astype(np.float64) - 127.0), 8, axis=1)[..., None]
    return vals.transpose(0, 1, 3, 2).reshape(g * 512, n)


def planes(y):
    n, m = y.shape
    v = y.astype(np.float32).astype(ml_dtypes.bfloat16).astype(np.float64).reshape(n // 32, 32, m)
    top = np.abs(v).max(1)
    byte = np.clip(np.where(top > 0, np.frexp(top)[1] - 1 + 127 - 7, 1), 1, 254)
    codes = (v * np.exp2(127.0 - byte)[:, None, :]).reshape(n, m).astype(np.float32).astype(ml_dtypes.float8_e4m3fn).view(np.uint8)
    words = codes.reshape(n // 512, 128, 4, m).transpose(0, 1, 3, 2)
    return np.ascontiguousarray(words), np.ascontiguousarray(byte.astype(np.uint8).reshape(n // 512, 16, m))


def silu(v):
    return v / (1.0 + np.exp(-np.maximum(v, -700.0)))


K, T, S, J = 512, 2048, 512, 512


def setup_inputs():
    n = np.random.standard_normal
    s = mx_kscale(K)[:, None]
    packed_xT = pack_weight(n((K, T)) * s)
    return {
        "x_words": packed_xT[0],
        "x_scales": packed_xT[1],
        "hT": (n((K, J)) / np.sqrt(K) / s).astype(np.float32),
        "offs": striped(np.random.permutation(T)[:S]),
    }


def reference(x_words, x_scales, hT, offs):
    xq = unpack_weight(x_words, x_scales)[:, unstriped(offs)]
    hTq = mxq(f64(hT), 0, "e4m3")
    out_0 = silu(xq.T @ hTq)
    return (out_0,) + planes(out_0)

@@ -1,0 +1,142 @@
+from contextlib import ExitStack
+
+import concourse.mybir as mybir
+
+K, T, S, J = 512, 2048, 512, 512
+FLOPS = 2 * K * S * J
+
+F32 = mybir.dt.float32
+BF16 = mybir.dt.bfloat16
+I32 = mybir.dt.int32
+U32 = mybir.dt.uint32
+U16 = mybir.dt.uint16
+U8 = mybir.dt.uint8
+FP8X4 = mybir.dt.float8_e4m3fn_x4
+SILU = mybir.ActivationFunctionType.Silu
+
+P = 128
+PACK = 4
+QUADS = 4
+CHUNKS = (128, 128, 128, 128)
+ON_SCALAR = (0, 1)
+
+
+def tile_picked_zdeja_silu_po_kernel(
+    tc, x_words, x_scales, hT, offs, out_0, out_1, out_2
+):
+    nc = tc.nc
+    starts = [sum(CHUNKS[:c]) for c in range(len(CHUNKS))]
+
+    with ExitStack() as ctx:
+        keep = ctx.enter_context(tc.tile_pool(name="keep", bufs=1))
+        psum = ctx.enter_context(tc.psum_pool(name="psum", bufs=1))
+
+        offsets = keep.tile([P, S // 16], U16, name="offsets")
+        nc.sync.dma_start(offsets[:], offs)
+
+        table_words = keep.tile([P, T], U32, name="table_words", align_bytes=64)
+        nc.sync.dma_start(
+            table_words[:].bitcast(I32),
+            x_words[0].rearrange("p n t -> p (n t)").bitcast(I32),
+        )
+
+        table_scales = keep.tile([P, T // 4], I32, name="table_scales", align_bytes=64)
+        nc.vector.memset(table_scales[:], 0)
+        for q in range(QUADS):
+            nc.scalar.dma_start(
+                table_scales[32 * q : 32 * q + 4, :],
+                x_scales[0, 4 * q : 4 * q + 4, :].bitcast(I32),
+            )
+
+        warm = keep.tile([P, 8], F32, name="warm")
+        warm_out = keep.tile([P, 8], F32, name="warm_out")
+        nc.vector.memset(warm[:], 0.0)
+        nc.scalar.activation(warm_out[:], warm[:], SILU)
+
+        h_rows = hT.rearrange("(p t) j -> p t j", t=PACK)
+        h_raw = []
+        for c, width in enumerate(CHUNKS):
+            raw = keep.tile([P, PACK, width], F32, name="h_raw%d" % c)
+            nc.sync.dma_start(raw[:], h_rows[:, :, starts[c] : starts[c] + width])
+            h_raw.append(raw)
+
+        picked_scales = keep.tile([P, S], U8, name="picked_scales", align_bytes=64)
+        nc.vector.tensor_copy(picked_scales[:], table_scales[:].bitcast(U8).indirect(offsets[:]))
+        x_scale = keep.tile([P, S], U8, name="x_scale", align_bytes=64)
+        nc.vector.tensor_copy(
+            x_scale[:].rearrange("p (t m) -> p t m", t=PACK),
+            picked_scales[:].rearrange("p (m t) -> p t m", t=PACK),
+        )
+        x_codes = keep.tile([P, S], U32, name="x_codes", align_bytes=64)
+        nc.vector.tensor_copy(
+            x_codes[:].rearrange("p (t m) -> p m t", t=PACK),
+            table_words[:].indirect(offsets[:]),
+        )
+
+        def interleave(engine_copy, grouped, planes):
+            engine_copy(
+                grouped[:].rearrange("p (c i) t -> p c t i", i=4),
+                planes[:].rearrange("p t (c i) -> p c t i", i=4),
+            )
+
+        y_rows = out_0.rearrange("(p t) j -> p t j", t=PACK)
+        words_out = out_1[0].rearrange("p n t -> p (n t)").bitcast(I32)
+        y_scale = keep.tile([P, J], U8, name="y_scale", align_bytes=64)
+
+        h_codes, h_scale, y_tiles = {}, {}, {}
+
+        def quantize_h(c):
+            width = CHUNKS[c]
+            grouped = keep.tile([P, width, PACK], BF16, name="h_grouped%d" % c, align_bytes=64)
+            interleave(nc.scalar.copy if c in ON_SCALAR else nc.vector.tensor_copy, grouped, h_raw[c])
+            h_codes[c] = keep.tile([P, width], U32, name="h_codes%d" % c, align_bytes=64)
+            h_scale[c] = keep.tile([P, width], U8, name="h_scale%d" % c, align_bytes=64)
+            nc.vector.quantize_mx(
+                out=h_codes[c][:].bitcast(FP8X4),
+                scales=h_scale[c][:],
+                in_=grouped[:].rearrange("p w t -> p (w t)"),
+            )
+
+        def multiply(c):
+            width = CHUNKS[c]
+            acc = psum.tile([P, PACK, width], F32, name="acc%d" % c)
+            for t in range(PACK):
+                rows = slice(t * P, (t + 1) * P)
+                nc.tensor.matmul_mx(
+                    out=acc[:, t, :],
+                    lhsT=x_codes[:, rows].bitcast(FP8X4),
+                    lhsT_scale=x_scale[:, rows],
+                    rhs=h_codes[c][:].bitcast(FP8X4),
+                    rhs_scale=h_scale[c][:],
+                    start=True,
+                    stop=True,
+                )
+            y_tiles[c] = keep.tile([P, PACK, width], F32, name="y%d" % c)
+            nc.scalar.activation(y_tiles[c][:], acc[:], SILU)
+            nc.sync.dma_start(y_rows[:, :, starts[c] : starts[c] + width], y_tiles[c][:])
+
+        def quantize_y(c):
+            width = CHUNKS[c]
+            cols = slice(starts[c], starts[c] + width)
+            grouped = keep.tile([P, width, PACK], BF16, name="y_grouped%d" % c, align_bytes=64)
+            interleave(nc.vector.tensor_copy, grouped, y_tiles[c])
+            codes = keep.tile([P, width], U32, name="y_codes%d" % c, align_bytes=64)
+            nc.vector.quantize_mx(
+                out=codes[:].bitcast(FP8X4),
+                scales=y_scale[:, cols],
+                in_=grouped[:].rearrange("p w t -> p (w t)"),
+            )
+            nc.sync.dma_start(words_out[:, cols], codes[:].bitcast(I32))
+
+        for c in range(len(CHUNKS)):
+            quantize_h(c)
+            multiply(c)
+        for c in range(len(CHUNKS)):
+            quantize_y(c)
+
+        for q in range(QUADS):
+            queue = nc.scalar if q % 2 else nc.sync
+            queue.dma_start(
+                out_2[0, 4 * q : 4 * q + 4, :].bitcast(I32),
+                y_scale[32 * q : 32 * q + 4, :].bitcast(I32),
+            )

@@ -18,7 +18,8 @@ P = 128
 PACK = 4
 QUADS = 4
 CHUNKS = (128, 128, 128, 128)
-ON_SCALAR = (0, 1)
+ON_SCALAR = (0, 1, 2)
+HEAD = 512
 
 
 def tile_picked_zdeja_silu_po_kernel(
@@ -35,18 +36,17 @@ def tile_picked_zdeja_silu_po_kernel(
         nc.sync.dma_start(offsets[:], offs)
 
         table_words = keep.tile([P, T], U32, name="table_words", align_bytes=64)
-        nc.sync.dma_start(
-            table_words[:].bitcast(I32),
-            x_words[0].rearrange("p n t -> p (n t)").bitcast(I32),
-        )
+        words_in = x_words[0].rearrange("p n t -> p (n t)").bitcast(I32)
+        nc.sync.dma_start(table_words[:, :HEAD].bitcast(I32), words_in[:, :HEAD])
 
         table_scales = keep.tile([P, T // 4], I32, name="table_scales", align_bytes=64)
         nc.vector.memset(table_scales[:], 0)
         for q in range(QUADS):
-            nc.scalar.dma_start(
+            nc.sync.dma_start(
                 table_scales[32 * q : 32 * q + 4, :],
                 x_scales[0, 4 * q : 4 * q + 4, :].bitcast(I32),
             )
+        nc.sync.dma_start(table_words[:, HEAD:].bitcast(I32), words_in[:, HEAD:])
 
         warm = keep.tile([P, 8], F32, name="warm")
         warm_out = keep.tile([P, 8], F32, name="warm_out")
@@ -87,7 +87,7 @@ def tile_picked_zdeja_silu_po_kernel(
 
         def quantize_h(c):
             width = CHUNKS[c]
-            grouped = keep.tile([P, width, PACK], BF16, name="h_grouped%d" % c, align_bytes=64)
+            grouped = keep.tile([P, width, PACK], BF16, name="h_grouped%d" % c, tag="grouped%d" % c, align_bytes=64)
             interleave(nc.scalar.copy if c in ON_SCALAR else nc.vector.tensor_copy, grouped, h_raw[c])
             h_codes[c] = keep.tile([P, width], U32, name="h_codes%d" % c, align_bytes=64)
             h_scale[c] = keep.tile([P, width], U8, name="h_scale%d" % c, align_bytes=64)
@@ -99,34 +99,36 @@ def tile_picked_zdeja_silu_po_kernel(
 
         def multiply(c):
             width = CHUNKS[c]
-            acc = psum.tile([P, PACK, width], F32, name="acc%d" % c)
-            for t in range(PACK):
-                rows = slice(t * P, (t + 1) * P)
-                nc.tensor.matmul_mx(
-                    out=acc[:, t, :],
-                    lhsT=x_codes[:, rows].bitcast(FP8X4),
-                    lhsT_scale=x_scale[:, rows],
-                    rhs=h_codes[c][:].bitcast(FP8X4),
-                    rhs_scale=h_scale[c][:],
-                    start=True,
-                    stop=True,
-                )
             y_tiles[c] = keep.tile([P, PACK, width], F32, name="y%d" % c)
-            nc.scalar.activation(y_tiles[c][:], acc[:], SILU)
+            for half in range(2):
+                acc = psum.tile([P, 2, width], F32, name="acc%d_%d" % (c, half))
+                for u in range(2):
+                    t = 2 * half + u
+                    rows = slice(t * P, (t + 1) * P)
+                    nc.tensor.matmul_mx(
+                        out=acc[:, u, :],
+                        lhsT=x_codes[:, rows].bitcast(FP8X4),
+                        lhsT_scale=x_scale[:, rows],
+                        rhs=h_codes[c][:].bitcast(FP8X4),
+                        rhs_scale=h_scale[c][:],
+                        start=True,
+                        stop=True,
+                    )
+                nc.scalar.activation(y_tiles[c][:, 2 * half : 2 * half + 2, :], acc[:], SILU)
             nc.sync.dma_start(y_rows[:, :, starts[c] : starts[c] + width], y_tiles[c][:])
+
+        y_codes = keep.tile([P, J], U32, name="y_codes", align_bytes=64)
 
         def quantize_y(c):
             width = CHUNKS[c]
             cols = slice(starts[c], starts[c] + width)
-            grouped = keep.tile([P, width, PACK], BF16, name="y_grouped%d" % c, align_bytes=64)
+            grouped = keep.tile([P, width, PACK], BF16, name="y_grouped%d" % c, tag="grouped%d" % (len(CHUNKS) - 1 - c), align_bytes=64)
             interleave(nc.vector.tensor_copy, grouped, y_tiles[c])
-            codes = keep.tile([P, width], U32, name="y_codes%d" % c, align_bytes=64)
             nc.vector.quantize_mx(
-                out=codes[:].bitcast(FP8X4),
+                out=y_codes[:, cols].bitcast(FP8X4),
                 scales=y_scale[:, cols],
                 in_=grouped[:].rearrange("p w t -> p (w t)"),
             )
-            nc.sync.dma_start(words_out[:, cols], codes[:].bitcast(I32))
 
         for c in range(len(CHUNKS)):
             quantize_h(c)
@@ -134,8 +136,9 @@ def tile_picked_zdeja_silu_po_kernel(
         for c in range(len(CHUNKS)):
             quantize_y(c)
 
+        nc.sync.dma_start(words_out, y_codes[:].bitcast(I32))
         for q in range(QUADS):
-            queue = nc.scalar if q % 2 else nc.sync
+            queue = nc.sync if q % 2 else nc.scalar
             queue.dma_start(
                 out_2[0, 4 * q : 4 * q + 4, :].bitcast(I32),
                 y_scale[32 * q : 32 * q + 4, :].bitcast(I32),

@@ -18,8 +18,8 @@ P = 128
 PACK = 4
 QUADS = 4
 CHUNKS = (128, 128, 128, 128)
-ON_SCALAR = (0, 1, 2)
-HEAD = 512
+SCALAR_COLS = (128, 128, 64, 0)
+HEAD = 768
 
 
 def tile_picked_zdeja_silu_po_kernel(
@@ -33,11 +33,11 @@ def tile_picked_zdeja_silu_po_kernel(
         psum = ctx.enter_context(tc.psum_pool(name="psum", bufs=1))
 
         offsets = keep.tile([P, S // 16], U16, name="offsets")
-        nc.sync.dma_start(offsets[:], offs)
 
         table_words = keep.tile([P, T], U32, name="table_words", align_bytes=64)
         words_in = x_words[0].rearrange("p n t -> p (n t)").bitcast(I32)
         nc.sync.dma_start(table_words[:, :HEAD].bitcast(I32), words_in[:, :HEAD])
+        nc.sync.dma_start(offsets[:], offs)
 
         table_scales = keep.tile([P, T // 4], I32, name="table_scales", align_bytes=64)
         nc.vector.memset(table_scales[:], 0)
@@ -75,8 +75,8 @@ def tile_picked_zdeja_silu_po_kernel(
 
         def interleave(engine_copy, grouped, planes):
             engine_copy(
-                grouped[:].rearrange("p (c i) t -> p c t i", i=4),
-                planes[:].rearrange("p t (c i) -> p c t i", i=4),
+                grouped.rearrange("p (c i) t -> p c t i", i=4),
+                planes.rearrange("p t (c i) -> p c t i", i=4),
             )
 
         y_rows = out_0.rearrange("(p t) j -> p t j", t=PACK)
@@ -88,7 +88,11 @@ def tile_picked_zdeja_silu_po_kernel(
         def quantize_h(c):
             width = CHUNKS[c]
             grouped = keep.tile([P, width, PACK], BF16, name="h_grouped%d" % c, tag="grouped%d" % c, align_bytes=64)
-            interleave(nc.scalar.copy if c in ON_SCALAR else nc.vector.tensor_copy, grouped, h_raw[c])
+            cut = SCALAR_COLS[c]
+            if cut:
+                interleave(nc.scalar.copy, grouped[:, :cut, :], h_raw[c][:, :, :cut])
+            if cut < width:
+                interleave(nc.vector.tensor_copy, grouped[:, cut:, :], h_raw[c][:, :, cut:])
             h_codes[c] = keep.tile([P, width], U32, name="h_codes%d" % c, align_bytes=64)
             h_scale[c] = keep.tile([P, width], U8, name="h_scale%d" % c, align_bytes=64)
             nc.vector.quantize_mx(
@@ -119,11 +123,14 @@ def tile_picked_zdeja_silu_po_kernel(
 
         y_codes = keep.tile([P, J], U32, name="y_codes", align_bytes=64)
 
-        def quantize_y(c):
-            width = CHUNKS[c]
-            cols = slice(starts[c], starts[c] + width)
-            grouped = keep.tile([P, width, PACK], BF16, name="y_grouped%d" % c, tag="grouped%d" % (len(CHUNKS) - 1 - c), align_bytes=64)
-            interleave(nc.vector.tensor_copy, grouped, y_tiles[c])
+        def quantize_y(group, tag):
+            width = sum(CHUNKS[c] for c in group)
+            first = starts[group[0]]
+            cols = slice(first, first + width)
+            grouped = keep.tile([P, width, PACK], BF16, name="y_grouped%d" % group[0], tag=tag, align_bytes=64)
+            for c in group:
+                lo = starts[c] - first
+                interleave(nc.vector.tensor_copy, grouped[:, lo : lo + CHUNKS[c], :], y_tiles[c][:])
             nc.vector.quantize_mx(
                 out=y_codes[:, cols].bitcast(FP8X4),
                 scales=y_scale[:, cols],
@@ -133,8 +140,9 @@ def tile_picked_zdeja_silu_po_kernel(
         for c in range(len(CHUNKS)):
             quantize_h(c)
             multiply(c)
-        for c in range(len(CHUNKS)):
-            quantize_y(c)
+        quantize_y((0, 1), "grouped3")
+        quantize_y((2,), "grouped2")
+        quantize_y((3,), "grouped1")
 
         nc.sync.dma_start(words_out, y_codes[:].bitcast(I32))
         for q in range(QUADS):

@@ -19,7 +19,7 @@ PACK = 4
 QUADS = 4
 CHUNKS = (128, 128, 128, 128)
 SCALAR_COLS = (128, 128, 64, 0)
-HEAD = 768
+HEAD = 640
 
 
 def tile_picked_zdeja_silu_po_kernel(
@@ -42,7 +42,8 @@ def tile_picked_zdeja_silu_po_kernel(
         table_scales = keep.tile([P, T // 4], I32, name="table_scales", align_bytes=64)
         nc.vector.memset(table_scales[:], 0)
         for q in range(QUADS):
-            nc.sync.dma_start(
+            queue = nc.scalar if q == QUADS - 1 else nc.sync
+            queue.dma_start(
                 table_scales[32 * q : 32 * q + 4, :],
                 x_scales[0, 4 * q : 4 * q + 4, :].bitcast(I32),
             )
@@ -50,7 +51,7 @@ def tile_picked_zdeja_silu_po_kernel(
 
         warm = keep.tile([P, 8], F32, name="warm")
         warm_out = keep.tile([P, 8], F32, name="warm_out")
-        nc.vector.memset(warm[:], 0.0)
+        nc.gpsimd.memset(warm[:], 0.0)
         nc.scalar.activation(warm_out[:], warm[:], SILU)
 
         h_rows = hT.rearrange("(p t) j -> p t j", t=PACK)
@@ -60,13 +61,17 @@ def tile_picked_zdeja_silu_po_kernel(
             nc.sync.dma_start(raw[:], h_rows[:, :, starts[c] : starts[c] + width])
             h_raw.append(raw)
 
-        picked_scales = keep.tile([P, S], U8, name="picked_scales", align_bytes=64)
-        nc.vector.tensor_copy(picked_scales[:], table_scales[:].bitcast(U8).indirect(offsets[:]))
-        x_scale = keep.tile([P, S], U8, name="x_scale", align_bytes=64)
-        nc.vector.tensor_copy(
-            x_scale[:].rearrange("p (t m) -> p t m", t=PACK),
-            picked_scales[:].rearrange("p (m t) -> p t m", t=PACK),
-        )
+        x_scale = keep.tile([P, PACK, P], U8, name="x_scale", align_bytes=64)
+        picked = []
+        for part in range(2):
+            picked.append(keep.tile([P, S // 2], U8, name="picked_scales%d" % part, align_bytes=64))
+            columns = offsets[:, part * S // 32 : (part + 1) * S // 32]
+            nc.vector.tensor_copy(picked[part][:], table_scales[:].bitcast(U8).indirect(columns))
+        for part in range(2):
+            nc.vector.tensor_copy(
+                x_scale[:, :, part * P // 2 : (part + 1) * P // 2],
+                picked[part][:].rearrange("p (m t) -> p t m", t=PACK),
+            )
         x_codes = keep.tile([P, S], U32, name="x_codes", align_bytes=64)
         nc.vector.tensor_copy(
             x_codes[:].rearrange("p (t m) -> p m t", t=PACK),
@@ -112,7 +117,7 @@ def tile_picked_zdeja_silu_po_kernel(
                     nc.tensor.matmul_mx(
                         out=acc[:, u, :],
                         lhsT=x_codes[:, rows].bitcast(FP8X4),
-                        lhsT_scale=x_scale[:, rows],
+                        lhsT_scale=x_scale[:, t, :],
                         rhs=h_codes[c][:].bitcast(FP8X4),
                         rhs_scale=h_scale[c][:],
                         start=True,
@@ -146,8 +151,7 @@ def tile_picked_zdeja_silu_po_kernel(
 
         nc.sync.dma_start(words_out, y_codes[:].bitcast(I32))
         for q in range(QUADS):
-            queue = nc.sync if q % 2 else nc.scalar
-            queue.dma_start(
+            nc.scalar.dma_start(
                 out_2[0, 4 * q : 4 * q + 4, :].bitcast(I32),
                 y_scale[32 * q : 32 * q + 4, :].bitcast(I32),
             )

@@ -19,7 +19,7 @@ PACK = 4
 QUADS = 4
 CHUNKS = (128, 128, 128, 128)
 SCALAR_COLS = (128, 128, 64, 0)
-HEAD = 640
+HEAD = 512
 
 
 def tile_picked_zdeja_silu_po_kernel(
@@ -42,7 +42,7 @@ def tile_picked_zdeja_silu_po_kernel(
         table_scales = keep.tile([P, T // 4], I32, name="table_scales", align_bytes=64)
         nc.vector.memset(table_scales[:], 0)
         for q in range(QUADS):
-            queue = nc.scalar if q == QUADS - 1 else nc.sync
+            queue = nc.scalar if q >= QUADS // 2 else nc.sync
             queue.dma_start(
                 table_scales[32 * q : 32 * q + 4, :],
                 x_scales[0, 4 * q : 4 * q + 4, :].bitcast(I32),
@@ -123,8 +123,12 @@ def tile_picked_zdeja_silu_po_kernel(
                         start=True,
                         stop=True,
                     )
-                nc.scalar.activation(y_tiles[c][:, 2 * half : 2 * half + 2, :], acc[:], SILU)
-            nc.sync.dma_start(y_rows[:, :, starts[c] : starts[c] + width], y_tiles[c][:])
+                pair = slice(2 * half, 2 * half + 2)
+                nc.scalar.activation(y_tiles[c][:, pair, :], acc[:], SILU)
+                if c == 0:
+                    nc.sync.dma_start(y_rows[:, pair, :width], y_tiles[c][:, pair, :])
+            if c:
+                nc.sync.dma_start(y_rows[:, :, starts[c] : starts[c] + width], y_tiles[c][:])
 
         y_codes = keep.tile([P, J], U32, name="y_codes", align_bytes=64)
 
@@ -147,11 +151,13 @@ def tile_picked_zdeja_silu_po_kernel(
             multiply(c)
         quantize_y((0, 1), "grouped3")
         quantize_y((2,), "grouped2")
+        nc.sync.dma_start(words_out[:, : starts[-1]], y_codes[:, : starts[-1]].bitcast(I32))
         quantize_y((3,), "grouped1")
 
-        nc.sync.dma_start(words_out, y_codes[:].bitcast(I32))
+        nc.sync.dma_start(words_out[:, starts[-1] :], y_codes[:, starts[-1] :].bitcast(I32))
         for q in range(QUADS):
-            nc.scalar.dma_start(
+            queue = nc.scalar if q else nc.sync
+            queue.dma_start(
                 out_2[0, 4 * q : 4 * q + 4, :].bitcast(I32),
                 y_scale[32 * q : 32 * q + 4, :].bitcast(I32),
             )

@@ -19,7 +19,7 @@ PACK = 4
 QUADS = 4
 CHUNKS = (128, 128, 128, 128)
 SCALAR_COLS = (128, 128, 64, 0)
-HEAD = 512
+HEAD = 640
 
 
 def tile_picked_zdeja_silu_po_kernel(
@@ -42,7 +42,7 @@ def tile_picked_zdeja_silu_po_kernel(
         table_scales = keep.tile([P, T // 4], I32, name="table_scales", align_bytes=64)
         nc.vector.memset(table_scales[:], 0)
         for q in range(QUADS):
-            queue = nc.scalar if q >= QUADS // 2 else nc.sync
+            queue = nc.scalar if q == QUADS - 1 else nc.sync
             queue.dma_start(
                 table_scales[32 * q : 32 * q + 4, :],
                 x_scales[0, 4 * q : 4 * q + 4, :].bitcast(I32),
@@ -132,29 +132,35 @@ def tile_picked_zdeja_silu_po_kernel(
 
         y_codes = keep.tile([P, J], U32, name="y_codes", align_bytes=64)
 
-        def quantize_y(group, tag):
-            width = sum(CHUNKS[c] for c in group)
-            first = starts[group[0]]
-            cols = slice(first, first + width)
-            grouped = keep.tile([P, width, PACK], BF16, name="y_grouped%d" % group[0], tag=tag, align_bytes=64)
-            for c in group:
-                lo = starts[c] - first
-                interleave(nc.vector.tensor_copy, grouped[:, lo : lo + CHUNKS[c], :], y_tiles[c][:])
+        y_grouped = {}
+        last = len(CHUNKS) - 1
+
+        def interleave_y(c):
+            y_grouped[c] = keep.tile(
+                [P, CHUNKS[c], PACK], BF16, name="y_grouped%d" % c, tag="grouped%d" % (last - c), align_bytes=64
+            )
+            interleave(nc.vector.tensor_copy, y_grouped[c][:], y_tiles[c][:])
+
+        def quantize_y(c):
+            cols = slice(starts[c], starts[c] + CHUNKS[c])
             nc.vector.quantize_mx(
                 out=y_codes[:, cols].bitcast(FP8X4),
                 scales=y_scale[:, cols],
-                in_=grouped[:].rearrange("p w t -> p (w t)"),
+                in_=y_grouped[c][:].rearrange("p w t -> p (w t)"),
             )
 
         for c in range(len(CHUNKS)):
             quantize_h(c)
             multiply(c)
-        quantize_y((0, 1), "grouped3")
-        quantize_y((2,), "grouped2")
-        nc.sync.dma_start(words_out[:, : starts[-1]], y_codes[:, : starts[-1]].bitcast(I32))
-        quantize_y((3,), "grouped1")
+        for c in range(len(CHUNKS)):
+            interleave_y(c)
+            if c:
+                quantize_y(c - 1)
+            if c == 2:
+                nc.sync.dma_start(words_out[:, : J // 2], y_codes[:, : J // 2].bitcast(I32))
+        quantize_y(last)
 
-        nc.sync.dma_start(words_out[:, starts[-1] :], y_codes[:, starts[-1] :].bitcast(I32))
+        nc.sync.dma_start(words_out[:, J // 2 :], y_codes[:, J // 2 :].bitcast(I32))
         for q in range(QUADS):
             queue = nc.scalar if q else nc.sync
             queue.dma_start(

@@ -106,29 +106,30 @@ def tile_picked_zdeja_silu_po_kernel(
                 in_=grouped[:].rearrange("p w t -> p (w t)"),
             )
 
-        def multiply(c):
+        y_wide = [keep.tile([P, PACK, J // 2], F32, name="y_wide%d" % side) for side in range(2)]
+        for c in range(len(CHUNKS)):
+            y_tiles[c] = y_wide[c // 2][:, :, (c % 2) * P : (c % 2 + 1) * P]
+
+        def multiply(c, half):
             width = CHUNKS[c]
-            y_tiles[c] = keep.tile([P, PACK, width], F32, name="y%d" % c)
-            for half in range(2):
-                acc = psum.tile([P, 2, width], F32, name="acc%d_%d" % (c, half))
-                for u in range(2):
-                    t = 2 * half + u
-                    rows = slice(t * P, (t + 1) * P)
-                    nc.tensor.matmul_mx(
-                        out=acc[:, u, :],
-                        lhsT=x_codes[:, rows].bitcast(FP8X4),
-                        lhsT_scale=x_scale[:, t, :],
-                        rhs=h_codes[c][:].bitcast(FP8X4),
-                        rhs_scale=h_scale[c][:],
-                        start=True,
-                        stop=True,
-                    )
-                pair = slice(2 * half, 2 * half + 2)
-                nc.scalar.activation(y_tiles[c][:, pair, :], acc[:], SILU)
-                if c == 0:
-                    nc.sync.dma_start(y_rows[:, pair, :width], y_tiles[c][:, pair, :])
-            if c:
-                nc.sync.dma_start(y_rows[:, :, starts[c] : starts[c] + width], y_tiles[c][:])
+            acc = psum.tile([P, 2, width], F32, name="acc%d_%d" % (c, half))
+            for u in range(2):
+                t = 2 * half + u
+                rows = slice(t * P, (t + 1) * P)
+                nc.tensor.matmul_mx(
+                    out=acc[:, u, :],
+                    lhsT=x_codes[:, rows].bitcast(FP8X4),
+                    lhsT_scale=x_scale[:, t, :],
+                    rhs=h_codes[c][:].bitcast(FP8X4),
+                    rhs_scale=h_scale[c][:],
+                    start=True,
+                    stop=True,
+                )
+            pair = slice(2 * half, 2 * half + 2)
+            nc.scalar.activation(y_tiles[c][:, pair, :], acc[:], SILU)
+            if c % 2:
+                side = c // 2
+                nc.sync.dma_start(y_rows[:, pair, side * J // 2 : (side + 1) * J // 2], y_wide[side][:, pair, :])
 
         y_codes = keep.tile([P, J], U32, name="y_codes", align_bytes=64)
 
@@ -139,7 +140,7 @@ def tile_picked_zdeja_silu_po_kernel(
             y_grouped[c] = keep.tile(
                 [P, CHUNKS[c], PACK], BF16, name="y_grouped%d" % c, tag="grouped%d" % (last - c), align_bytes=64
             )
-            interleave(nc.vector.tensor_copy, y_grouped[c][:], y_tiles[c][:])
+            interleave(nc.vector.tensor_copy, y_grouped[c][:], y_tiles[c])
 
         def quantize_y(c):
             cols = slice(starts[c], starts[c] + CHUNKS[c])
@@ -149,18 +150,19 @@ def tile_picked_zdeja_silu_po_kernel(
                 in_=y_grouped[c][:].rearrange("p w t -> p (w t)"),
             )
 
-        for c in range(len(CHUNKS)):
-            quantize_h(c)
-            multiply(c)
+        for side in range(2):
+            for c in (2 * side, 2 * side + 1):
+                quantize_h(c)
+                multiply(c, 0)
+            for c in (2 * side, 2 * side + 1):
+                multiply(c, 1)
         for c in range(len(CHUNKS)):
             interleave_y(c)
             if c:
                 quantize_y(c - 1)
-            if c == 2:
-                nc.sync.dma_start(words_out[:, : J // 2], y_codes[:, : J // 2].bitcast(I32))
         quantize_y(last)
 
-        nc.sync.dma_start(words_out[:, J // 2 :], y_codes[:, J // 2 :].bitcast(I32))
+        nc.sync.dma_start(words_out, y_codes[:].bitcast(I32))
         for q in range(QUADS):
             queue = nc.scalar if q else nc.sync
             queue.dma_start(

@@ -42,7 +42,7 @@ def tile_picked_zdeja_silu_po_kernel(
         table_scales = keep.tile([P, T // 4], I32, name="table_scales", align_bytes=64)
         nc.vector.memset(table_scales[:], 0)
         for q in range(QUADS):
-            queue = nc.scalar if q == QUADS - 1 else nc.sync
+            queue = nc.scalar if q >= QUADS // 2 else nc.sync
             queue.dma_start(
                 table_scales[32 * q : 32 * q + 4, :],
                 x_scales[0, 4 * q : 4 * q + 4, :].bitcast(I32),
@@ -88,7 +88,8 @@ def tile_picked_zdeja_silu_po_kernel(
         words_out = out_1[0].rearrange("p n t -> p (n t)").bitcast(I32)
         y_scale = keep.tile([P, J], U8, name="y_scale", align_bytes=64)
 
-        h_codes, h_scale, y_tiles = {}, {}, {}
+        h_codes, h_scale = {}, {}
+        last = len(CHUNKS) - 1
 
         def quantize_h(c):
             width = CHUNKS[c]
@@ -106,9 +107,10 @@ def tile_picked_zdeja_silu_po_kernel(
                 in_=grouped[:].rearrange("p w t -> p (w t)"),
             )
 
-        y_wide = [keep.tile([P, PACK, J // 2], F32, name="y_wide%d" % side) for side in range(2)]
-        for c in range(len(CHUNKS)):
-            y_tiles[c] = y_wide[c // 2][:, :, (c % 2) * P : (c % 2 + 1) * P]
+        y_first = keep.tile([P, PACK, P], F32, name="y_first")
+        y_mid = keep.tile([P, PACK, P], F32, name="y_mid")
+        y_last = keep.tile([P, PACK, 2 * P], F32, name="y_last")
+        y_tiles = [y_first[:], y_mid[:], y_last[:, :, :P], y_last[:, :, P:]]
 
         def multiply(c, half):
             width = CHUNKS[c]
@@ -126,21 +128,29 @@ def tile_picked_zdeja_silu_po_kernel(
                     stop=True,
                 )
             pair = slice(2 * half, 2 * half + 2)
-            nc.scalar.activation(y_tiles[c][:, pair, :], acc[:], SILU)
-            if c % 2:
-                side = c // 2
-                nc.sync.dma_start(y_rows[:, pair, side * J // 2 : (side + 1) * J // 2], y_wide[side][:, pair, :])
+            parts = 2 if (c, half) == (last, 1) else 1
+            for part in range(parts):
+                cols = slice(part * width // parts, (part + 1) * width // parts)
+                nc.scalar.activation(y_tiles[c][:, pair, cols], acc[:, :, cols], SILU)
+            if c == 0:
+                nc.sync.dma_start(y_rows[:, pair, :P], y_first[:, pair, :])
+            if (c, half) == (1, 1):
+                nc.sync.dma_start(y_rows[:, :, P : 2 * P], y_mid[:])
+            if c == last:
+                nc.sync.dma_start(y_rows[:, pair, 2 * P :], y_last[:, pair, :])
 
         y_codes = keep.tile([P, J], U32, name="y_codes", align_bytes=64)
 
         y_grouped = {}
-        last = len(CHUNKS) - 1
 
         def interleave_y(c):
             y_grouped[c] = keep.tile(
                 [P, CHUNKS[c], PACK], BF16, name="y_grouped%d" % c, tag="grouped%d" % (last - c), align_bytes=64
             )
-            interleave(nc.vector.tensor_copy, y_grouped[c][:], y_tiles[c])
+            parts = 2 if c == last else 1
+            for part in range(parts):
+                cols = slice(part * CHUNKS[c] // parts, (part + 1) * CHUNKS[c] // parts)
+                interleave(nc.vector.tensor_copy, y_grouped[c][:, cols, :], y_tiles[c][:, :, cols])
 
         def quantize_y(c):
             cols = slice(starts[c], starts[c] + CHUNKS[c])
@@ -150,19 +160,21 @@ def tile_picked_zdeja_silu_po_kernel(
                 in_=y_grouped[c][:].rearrange("p w t -> p (w t)"),
             )
 
-        for side in range(2):
-            for c in (2 * side, 2 * side + 1):
+        for group in ((0,), (1,), (2, 3)):
+            for c in group:
                 quantize_h(c)
                 multiply(c, 0)
-            for c in (2 * side, 2 * side + 1):
+            for c in group:
                 multiply(c, 1)
         for c in range(len(CHUNKS)):
             interleave_y(c)
             if c:
                 quantize_y(c - 1)
+            if c == 2:
+                nc.sync.dma_start(words_out[:, : J // 2], y_codes[:, : J // 2].bitcast(I32))
         quantize_y(last)
 
-        nc.sync.dma_start(words_out, y_codes[:].bitcast(I32))
+        nc.sync.dma_start(words_out[:, J // 2 :], y_codes[:, J // 2 :].bitcast(I32))
         for q in range(QUADS):
             queue = nc.scalar if q else nc.sync
             queue.dma_start(

@@ -42,7 +42,7 @@ def tile_picked_zdeja_silu_po_kernel(
         table_scales = keep.tile([P, T // 4], I32, name="table_scales", align_bytes=64)
         nc.vector.memset(table_scales[:], 0)
         for q in range(QUADS):
-            queue = nc.scalar if q >= QUADS // 2 else nc.sync
+            queue = nc.scalar if q == QUADS - 1 else nc.sync
             queue.dma_start(
                 table_scales[32 * q : 32 * q + 4, :],
                 x_scales[0, 4 * q : 4 * q + 4, :].bitcast(I32),
@@ -51,7 +51,7 @@ def tile_picked_zdeja_silu_po_kernel(
 
         warm = keep.tile([P, 8], F32, name="warm")
         warm_out = keep.tile([P, 8], F32, name="warm_out")
-        nc.gpsimd.memset(warm[:], 0.0)
+        nc.vector.memset(warm[:], 0.0)
         nc.scalar.activation(warm_out[:], warm[:], SILU)
 
         h_rows = hT.rearrange("(p t) j -> p t j", t=PACK)
@@ -136,8 +136,8 @@ def tile_picked_zdeja_silu_po_kernel(
                 nc.sync.dma_start(y_rows[:, pair, :P], y_first[:, pair, :])
             if (c, half) == (1, 1):
                 nc.sync.dma_start(y_rows[:, :, P : 2 * P], y_mid[:])
-            if c == last:
-                nc.sync.dma_start(y_rows[:, pair, 2 * P :], y_last[:, pair, :])
+            if c > 1 and half:
+                nc.sync.dma_start(y_rows[:, :, c * P : (c + 1) * P], y_tiles[c])
 
         y_codes = keep.tile([P, J], U32, name="y_codes", align_bytes=64)
 
@@ -160,7 +160,7 @@ def tile_picked_zdeja_silu_po_kernel(
                 in_=y_grouped[c][:].rearrange("p w t -> p (w t)"),
             )
 
-        for group in ((0,), (1,), (2, 3)):
+        for group in ((0,), (1,), (2,), (3,)):
             for c in group:
                 quantize_h(c)
                 multiply(c, 0)

@@ -132,10 +132,8 @@ def tile_picked_zdeja_silu_po_kernel(
             for part in range(parts):
                 cols = slice(part * width // parts, (part + 1) * width // parts)
                 nc.scalar.activation(y_tiles[c][:, pair, cols], acc[:, :, cols], SILU)
-            if c == 0:
-                nc.sync.dma_start(y_rows[:, pair, :P], y_first[:, pair, :])
-            if (c, half) == (1, 1):
-                nc.sync.dma_start(y_rows[:, :, P : 2 * P], y_mid[:])
+            if c < 2:
+                nc.sync.dma_start(y_rows[:, pair, c * P : (c + 1) * P], y_tiles[c][:, pair, :])
             if c > 1 and half:
                 nc.sync.dma_start(y_rows[:, :, c * P : (c + 1) * P], y_tiles[c])
 

@@ -17,23 +17,29 @@ SILU = mybir.ActivationFunctionType.Silu
 P = 128
 PACK = 4
 QUADS = 4
-CHUNKS = (128, 128, 128, 128)
-SCALAR_COLS = (128, 128, 64, 0)
-HEAD = 640
+CHUNKS = J // P
+HEAD = 864
+SCALAR_COLS = (128, 128, 128, 0)
 
 
 def tile_picked_zdeja_silu_po_kernel(
     tc, x_words, x_scales, hT, offs, out_0, out_1, out_2
 ):
     nc = tc.nc
-    starts = [sum(CHUNKS[:c]) for c in range(len(CHUNKS))]
+    last = CHUNKS - 1
 
     with ExitStack() as ctx:
         keep = ctx.enter_context(tc.tile_pool(name="keep", bufs=1))
         psum = ctx.enter_context(tc.psum_pool(name="psum", bufs=1))
 
-        offsets = keep.tile([P, S // 16], U16, name="offsets")
+        h_rows = hT.rearrange("(p t) j -> p t j", t=PACK)
+        h_raw = []
 
+        def load_h(c):
+            h_raw.append(keep.tile([P, PACK, P], F32, name="h_raw%d" % c, tag="raw%d" % c, align_bytes=64))
+            nc.sync.dma_start(h_raw[c][:], h_rows[:, :, c * P : (c + 1) * P])
+
+        offsets = keep.tile([P, S // 16], U16, name="offsets")
         table_words = keep.tile([P, T], U32, name="table_words", align_bytes=64)
         words_in = x_words[0].rearrange("p n t -> p (n t)").bitcast(I32)
         nc.sync.dma_start(table_words[:, :HEAD].bitcast(I32), words_in[:, :HEAD])
@@ -42,11 +48,12 @@ def tile_picked_zdeja_silu_po_kernel(
         table_scales = keep.tile([P, T // 4], I32, name="table_scales", align_bytes=64)
         nc.vector.memset(table_scales[:], 0)
         for q in range(QUADS):
-            queue = nc.scalar if q == QUADS - 1 else nc.sync
+            queue = nc.scalar if q >= 3 else nc.sync
             queue.dma_start(
                 table_scales[32 * q : 32 * q + 4, :],
                 x_scales[0, 4 * q : 4 * q + 4, :].bitcast(I32),
             )
+        load_h(0)
         nc.sync.dma_start(table_words[:, HEAD:].bitcast(I32), words_in[:, HEAD:])
 
         warm = keep.tile([P, 8], F32, name="warm")
@@ -54,118 +61,128 @@ def tile_picked_zdeja_silu_po_kernel(
         nc.vector.memset(warm[:], 0.0)
         nc.scalar.activation(warm_out[:], warm[:], SILU)
 
-        h_rows = hT.rearrange("(p t) j -> p t j", t=PACK)
-        h_raw = []
-        for c, width in enumerate(CHUNKS):
-            raw = keep.tile([P, PACK, width], F32, name="h_raw%d" % c)
-            nc.sync.dma_start(raw[:], h_rows[:, :, starts[c] : starts[c] + width])
-            h_raw.append(raw)
+        for c in range(1, CHUNKS):
+            load_h(c)
 
-        x_scale = keep.tile([P, PACK, P], U8, name="x_scale", align_bytes=64)
-        picked = []
-        for part in range(2):
-            picked.append(keep.tile([P, S // 2], U8, name="picked_scales%d" % part, align_bytes=64))
-            columns = offsets[:, part * S // 32 : (part + 1) * S // 32]
-            nc.vector.tensor_copy(picked[part][:], table_scales[:].bitcast(U8).indirect(columns))
-        for part in range(2):
-            nc.vector.tensor_copy(
-                x_scale[:, :, part * P // 2 : (part + 1) * P // 2],
-                picked[part][:].rearrange("p (m t) -> p t m", t=PACK),
-            )
-        x_codes = keep.tile([P, S], U32, name="x_codes", align_bytes=64)
-        nc.vector.tensor_copy(
-            x_codes[:].rearrange("p (t m) -> p m t", t=PACK),
-            table_words[:].indirect(offsets[:]),
-        )
-
-        def interleave(engine_copy, grouped, planes):
-            engine_copy(
+        def interleave(engine_op, grouped, planes):
+            engine_op(
                 grouped.rearrange("p (c i) t -> p c t i", i=4),
                 planes.rearrange("p t (c i) -> p c t i", i=4),
             )
 
-        y_rows = out_0.rearrange("(p t) j -> p t j", t=PACK)
-        words_out = out_1[0].rearrange("p n t -> p (n t)").bitcast(I32)
-        y_scale = keep.tile([P, J], U8, name="y_scale", align_bytes=64)
-
         h_codes, h_scale = {}, {}
-        last = len(CHUNKS) - 1
 
         def quantize_h(c):
-            width = CHUNKS[c]
-            grouped = keep.tile([P, width, PACK], BF16, name="h_grouped%d" % c, tag="grouped%d" % c, align_bytes=64)
+            grouped = keep.tile([P, P, PACK], BF16, name="h_grouped%d" % c, tag="grouped%d" % c, align_bytes=64)
             cut = SCALAR_COLS[c]
             if cut:
                 interleave(nc.scalar.copy, grouped[:, :cut, :], h_raw[c][:, :, :cut])
-            if cut < width:
+            if cut < P:
                 interleave(nc.vector.tensor_copy, grouped[:, cut:, :], h_raw[c][:, :, cut:])
-            h_codes[c] = keep.tile([P, width], U32, name="h_codes%d" % c, align_bytes=64)
-            h_scale[c] = keep.tile([P, width], U8, name="h_scale%d" % c, align_bytes=64)
+            h_codes[c] = keep.tile([P, P], U32, name="h_codes%d" % c, align_bytes=64)
+            h_scale[c] = keep.tile([P, P], U8, name="h_scale%d" % c, align_bytes=64)
             nc.vector.quantize_mx(
                 out=h_codes[c][:].bitcast(FP8X4),
                 scales=h_scale[c][:],
                 in_=grouped[:].rearrange("p w t -> p (w t)"),
             )
 
-        y_first = keep.tile([P, PACK, P], F32, name="y_first")
-        y_mid = keep.tile([P, PACK, P], F32, name="y_mid")
-        y_last = keep.tile([P, PACK, 2 * P], F32, name="y_last")
-        y_tiles = [y_first[:], y_mid[:], y_last[:, :, :P], y_last[:, :, P:]]
+        picked = []
+        for part in range(2):
+            picked.append(keep.tile([P, S // 2], U8, name="picked_scales%d" % part, align_bytes=64))
+            columns = offsets[:, part * S // 32 : (part + 1) * S // 32]
+            nc.vector.tensor_copy(picked[part][:], table_scales[:].bitcast(U8).indirect(columns))
 
-        def multiply(c, half):
-            width = CHUNKS[c]
-            acc = psum.tile([P, 2, width], F32, name="acc%d_%d" % (c, half))
-            for u in range(2):
-                t = 2 * half + u
-                rows = slice(t * P, (t + 1) * P)
-                nc.tensor.matmul_mx(
-                    out=acc[:, u, :],
-                    lhsT=x_codes[:, rows].bitcast(FP8X4),
-                    lhsT_scale=x_scale[:, t, :],
-                    rhs=h_codes[c][:].bitcast(FP8X4),
-                    rhs_scale=h_scale[c][:],
-                    start=True,
-                    stop=True,
+        x_scale = {}
+
+        def deal_scales(half, tag):
+            x_scale[half] = keep.tile([P, 2, P], U8, name="x_scale%d" % half, tag=tag, align_bytes=64)
+            for part in range(2):
+                nc.vector.tensor_copy(
+                    x_scale[half][:, :, part * P // 2 : (part + 1) * P // 2],
+                    picked[part][:].rearrange("p (m t) -> p t m", t=PACK)[:, 2 * half : 2 * half + 2, :],
                 )
-            pair = slice(2 * half, 2 * half + 2)
-            parts = 2 if (c, half) == (last, 1) else 1
-            for part in range(parts):
-                cols = slice(part * width // parts, (part + 1) * width // parts)
-                nc.scalar.activation(y_tiles[c][:, pair, cols], acc[:, :, cols], SILU)
-            if c < 2:
-                nc.sync.dma_start(y_rows[:, pair, c * P : (c + 1) * P], y_tiles[c][:, pair, :])
-            if c > 1 and half:
-                nc.sync.dma_start(y_rows[:, :, c * P : (c + 1) * P], y_tiles[c])
 
+        deal_scales(0, "x_scale0")
+        quantize_h(0)
+        x_codes = keep.tile([P, S], U32, name="x_codes", align_bytes=64)
+        nc.vector.tensor_copy(
+            x_codes[:].rearrange("p (t m) -> p m t", t=PACK),
+            table_words[:].indirect(offsets[:]),
+        )
+        deal_scales(1, "raw1")
+        for c in range(1, CHUNKS):
+            quantize_h(c)
+
+        y_rows = out_0.rearrange("(p t) j -> p t j", t=PACK)
+        words_out = out_1[0].rearrange("p n t -> p (n t)").bitcast(I32)
+        y_scale = keep.tile([P, J], U8, name="y_scale", align_bytes=64)
         y_codes = keep.tile([P, J], U32, name="y_codes", align_bytes=64)
+        y_front = keep.tile([P, PACK, 2 * P], F32, name="y_front", tag="raw2", align_bytes=64)
+        y_back = keep.tile([P, PACK, 2 * P], F32, name="y_back")
+        y_tiles = [y_front[:, :, :P], y_front[:, :, P:], y_back[:, :, :P], y_back[:, :, P:]]
+
+        def product(acc, c, t):
+            nc.tensor.matmul_mx(
+                out=acc,
+                lhsT=x_codes[:, t * P : (t + 1) * P].bitcast(FP8X4),
+                lhsT_scale=x_scale[t // 2][:, t % 2, :],
+                rhs=h_codes[c][:].bitcast(FP8X4),
+                rhs_scale=h_scale[c][:],
+                start=True,
+                stop=True,
+            )
+
+        def multiply(c, half, parts=1):
+            acc = psum.tile([P, 2, P], F32, name="acc%d_%d" % (c, half), tag="bank%d" % ((2 * c + half) % 7))
+            for u in range(2):
+                product(acc[:, u, :], c, 2 * half + u)
+            for part in range(parts):
+                cols = slice(part * P // parts, (part + 1) * P // parts)
+                nc.scalar.activation(y_tiles[c][:, 2 * half : 2 * half + 2, cols], acc[:, :, cols], SILU)
+
+        def multiply_singly(c):
+            for t in range(2):
+                acc = psum.tile([P, P], F32, name="acc_single%d" % t, tag="bank%d" % (7 * t))
+                product(acc[:], c, t)
+                nc.scalar.activation(y_tiles[c][:, t, :], acc[:], SILU)
+
+        def store_y(tiles, cols):
+            source = y_front if cols.start < 2 * P else y_back
+            local = slice(cols.start % (2 * P), cols.start % (2 * P) + cols.stop - cols.start)
+            nc.sync.dma_start(y_rows[:, tiles, cols], source[:, tiles, local])
 
         y_grouped = {}
 
-        def interleave_y(c):
+        def interleave_y(c, parts=1):
             y_grouped[c] = keep.tile(
-                [P, CHUNKS[c], PACK], BF16, name="y_grouped%d" % c, tag="grouped%d" % (last - c), align_bytes=64
+                [P, P, PACK], BF16, name="y_grouped%d" % c, tag="grouped%d" % (last - c), align_bytes=64
             )
-            parts = 2 if c == last else 1
             for part in range(parts):
-                cols = slice(part * CHUNKS[c] // parts, (part + 1) * CHUNKS[c] // parts)
+                cols = slice(part * P // parts, (part + 1) * P // parts)
                 interleave(nc.vector.tensor_copy, y_grouped[c][:, cols, :], y_tiles[c][:, :, cols])
 
         def quantize_y(c):
-            cols = slice(starts[c], starts[c] + CHUNKS[c])
+            cols = slice(c * P, (c + 1) * P)
             nc.vector.quantize_mx(
                 out=y_codes[:, cols].bitcast(FP8X4),
                 scales=y_scale[:, cols],
                 in_=y_grouped[c][:].rearrange("p w t -> p (w t)"),
             )
 
-        for group in ((0,), (1,), (2,), (3,)):
-            for c in group:
-                quantize_h(c)
-                multiply(c, 0)
-            for c in group:
-                multiply(c, 1)
-        for c in range(len(CHUNKS)):
-            interleave_y(c)
+        for c in range(CHUNKS):
+            cols = slice(c * P, (c + 1) * P)
+            for half in range(2):
+                if (c, half) == (0, 0):
+                    multiply_singly(c)
+                else:
+                    multiply(c, half, 2 if (c, half) == (last, 1) else 1)
+                if c < 2:
+                    store_y(slice(2 * half, 2 * half + 2), cols)
+            if c >= 2:
+                store_y(slice(0, PACK), cols)
+        for c in range(CHUNKS):
+            interleave_y(c, 2 if c == last else 1)
             if c:
                 quantize_y(c - 1)
             if c == 2:

@@ -18,7 +18,7 @@ P = 128
 PACK = 4
 QUADS = 4
 CHUNKS = J // P
-HEAD = 864
+HEAD = 768
 SCALAR_COLS = (128, 128, 128, 0)
 
 
@@ -191,7 +191,7 @@ def tile_picked_zdeja_silu_po_kernel(
 
         nc.sync.dma_start(words_out[:, J // 2 :], y_codes[:, J // 2 :].bitcast(I32))
         for q in range(QUADS):
-            queue = nc.scalar if q else nc.sync
+            queue = nc.scalar if q >= QUADS // 2 else nc.sync
             queue.dma_start(
                 out_2[0, 4 * q : 4 * q + 4, :].bitcast(I32),
                 y_scale[32 * q : 32 * q + 4, :].bitcast(I32),

@@ -18,7 +18,7 @@ P = 128
 PACK = 4
 QUADS = 4
 CHUNKS = J // P
-HEAD = 768
+HEAD = 704
 SCALAR_COLS = (128, 128, 128, 0)
 
 
@@ -191,7 +191,7 @@ def tile_picked_zdeja_silu_po_kernel(
 
         nc.sync.dma_start(words_out[:, J // 2 :], y_codes[:, J // 2 :].bitcast(I32))
         for q in range(QUADS):
-            queue = nc.scalar if q >= QUADS // 2 else nc.sync
+            queue = nc.scalar if q == QUADS - 1 else nc.sync
             queue.dma_start(
                 out_2[0, 4 * q : 4 * q + 4, :].bitcast(I32),
                 y_scale[32 * q : 32 * q + 4, :].bitcast(I32),

@@ -18,8 +18,7 @@ P = 128
 PACK = 4
 QUADS = 4
 CHUNKS = J // P
-HEAD = 704
-SCALAR_COLS = (128, 128, 128, 0)
+SCALAR_COLS = (0, 128, 128, 0)
 
 
 def tile_picked_zdeja_silu_po_kernel(
@@ -42,7 +41,7 @@ def tile_picked_zdeja_silu_po_kernel(
         offsets = keep.tile([P, S // 16], U16, name="offsets")
         table_words = keep.tile([P, T], U32, name="table_words", align_bytes=64)
         words_in = x_words[0].rearrange("p n t -> p (n t)").bitcast(I32)
-        nc.sync.dma_start(table_words[:, :HEAD].bitcast(I32), words_in[:, :HEAD])
+        load_h(0)
         nc.sync.dma_start(offsets[:], offs)
 
         table_scales = keep.tile([P, T // 4], I32, name="table_scales", align_bytes=64)
@@ -53,8 +52,7 @@ def tile_picked_zdeja_silu_po_kernel(
                 table_scales[32 * q : 32 * q + 4, :],
                 x_scales[0, 4 * q : 4 * q + 4, :].bitcast(I32),
             )
-        load_h(0)
-        nc.sync.dma_start(table_words[:, HEAD:].bitcast(I32), words_in[:, HEAD:])
+        nc.sync.dma_start(table_words[:].bitcast(I32), words_in)
 
         warm = keep.tile([P, 8], F32, name="warm")
         warm_out = keep.tile([P, 8], F32, name="warm_out")
@@ -87,6 +85,7 @@ def tile_picked_zdeja_silu_po_kernel(
                 in_=grouped[:].rearrange("p w t -> p (w t)"),
             )
 
+        quantize_h(0)
         picked = []
         for part in range(2):
             picked.append(keep.tile([P, S // 2], U8, name="picked_scales%d" % part, align_bytes=64))
@@ -104,7 +103,6 @@ def tile_picked_zdeja_silu_po_kernel(
                 )
 
         deal_scales(0, "x_scale0")
-        quantize_h(0)
         x_codes = keep.tile([P, S], U32, name="x_codes", align_bytes=64)
         nc.vector.tensor_copy(
             x_codes[:].rearrange("p (t m) -> p m t", t=PACK),

@@ -86,29 +86,16 @@ def tile_picked_zdeja_silu_po_kernel(
             )
 
         quantize_h(0)
-        picked = []
-        for part in range(2):
-            picked.append(keep.tile([P, S // 2], U8, name="picked_scales%d" % part, align_bytes=64))
-            columns = offsets[:, part * S // 32 : (part + 1) * S // 32]
-            nc.vector.tensor_copy(picked[part][:], table_scales[:].bitcast(U8).indirect(columns))
-
-        x_scale = {}
-
-        def deal_scales(half, tag):
-            x_scale[half] = keep.tile([P, 2, P], U8, name="x_scale%d" % half, tag=tag, align_bytes=64)
-            for part in range(2):
-                nc.vector.tensor_copy(
-                    x_scale[half][:, :, part * P // 2 : (part + 1) * P // 2],
-                    picked[part][:].rearrange("p (m t) -> p t m", t=PACK)[:, 2 * half : 2 * half + 2, :],
-                )
-
-        deal_scales(0, "x_scale0")
+        x_scale = keep.tile([P, S], U8, name="x_scale", align_bytes=64)
+        nc.vector.tensor_copy(
+            x_scale[:].rearrange("p (t m) -> p m t", t=PACK),
+            table_scales[:].bitcast(U8).indirect(offsets[:]),
+        )
         x_codes = keep.tile([P, S], U32, name="x_codes", align_bytes=64)
         nc.vector.tensor_copy(
             x_codes[:].rearrange("p (t m) -> p m t", t=PACK),
             table_words[:].indirect(offsets[:]),
         )
-        deal_scales(1, "raw1")
         for c in range(1, CHUNKS):
             quantize_h(c)
 
@@ -124,7 +111,7 @@ def tile_picked_zdeja_silu_po_kernel(
             nc.tensor.matmul_mx(
                 out=acc,
                 lhsT=x_codes[:, t * P : (t + 1) * P].bitcast(FP8X4),
-                lhsT_scale=x_scale[t // 2][:, t % 2, :],
+                lhsT_scale=x_scale[:, t * P : (t + 1) * P],
                 rhs=h_codes[c][:].bitcast(FP8X4),
                 rhs_scale=h_scale[c][:],
                 start=True,

@@ -86,11 +86,13 @@ def tile_picked_zdeja_silu_po_kernel(
             )
 
         quantize_h(0)
-        x_scale = keep.tile([P, S], U8, name="x_scale", align_bytes=64)
+        picked = keep.tile([P, S], U8, name="picked", align_bytes=64)
         nc.vector.tensor_copy(
-            x_scale[:].rearrange("p (t m) -> p m t", t=PACK),
+            picked[:].rearrange("p (c t i) -> p c i t", t=PACK, i=4),
             table_scales[:].bitcast(U8).indirect(offsets[:]),
         )
+        x_scale = keep.tile([P, PACK, P // 4], I32, name="x_scale", align_bytes=64)
+        nc.vector.tensor_copy(x_scale[:], picked[:].bitcast(I32).rearrange("p (c t) -> p t c", t=PACK))
         x_codes = keep.tile([P, S], U32, name="x_codes", align_bytes=64)
         nc.vector.tensor_copy(
             x_codes[:].rearrange("p (t m) -> p m t", t=PACK),
@@ -111,7 +113,7 @@ def tile_picked_zdeja_silu_po_kernel(
             nc.tensor.matmul_mx(
                 out=acc,
                 lhsT=x_codes[:, t * P : (t + 1) * P].bitcast(FP8X4),
-                lhsT_scale=x_scale[:, t * P : (t + 1) * P],
+                lhsT_scale=x_scale[:, t, :].bitcast(U8),
                 rhs=h_codes[c][:].bitcast(FP8X4),
                 rhs_scale=h_scale[c][:],
                 start=True,

@@ -18,6 +18,7 @@ P = 128
 PACK = 4
 QUADS = 4
 CHUNKS = J // P
+DMA_ALIGN = 512
 SCALAR_COLS = (0, 128, 128, 0)
 
 
@@ -35,16 +36,16 @@ def tile_picked_zdeja_silu_po_kernel(
         h_raw = []
 
         def load_h(c):
-            h_raw.append(keep.tile([P, PACK, P], F32, name="h_raw%d" % c, tag="raw%d" % c, align_bytes=64))
+            h_raw.append(keep.tile([P, PACK, P], F32, name="h_raw%d" % c, tag="raw%d" % c, align_bytes=DMA_ALIGN))
             nc.sync.dma_start(h_raw[c][:], h_rows[:, :, c * P : (c + 1) * P])
 
         offsets = keep.tile([P, S // 16], U16, name="offsets")
-        table_words = keep.tile([P, T], U32, name="table_words", align_bytes=64)
+        table_words = keep.tile([P, T], U32, name="table_words", align_bytes=DMA_ALIGN)
         words_in = x_words[0].rearrange("p n t -> p (n t)").bitcast(I32)
         load_h(0)
         nc.sync.dma_start(offsets[:], offs)
 
-        table_scales = keep.tile([P, T // 4], I32, name="table_scales", align_bytes=64)
+        table_scales = keep.tile([P, T // 4], I32, name="table_scales", align_bytes=DMA_ALIGN)
         nc.vector.memset(table_scales[:], 0)
         for q in range(QUADS):
             queue = nc.scalar if q >= 3 else nc.sync
@@ -103,10 +104,10 @@ def tile_picked_zdeja_silu_po_kernel(
 
         y_rows = out_0.rearrange("(p t) j -> p t j", t=PACK)
         words_out = out_1[0].rearrange("p n t -> p (n t)").bitcast(I32)
-        y_scale = keep.tile([P, J], U8, name="y_scale", align_bytes=64)
-        y_codes = keep.tile([P, J], U32, name="y_codes", align_bytes=64)
-        y_front = keep.tile([P, PACK, 2 * P], F32, name="y_front", tag="raw2", align_bytes=64)
-        y_back = keep.tile([P, PACK, 2 * P], F32, name="y_back")
+        y_scale = keep.tile([P, J], U8, name="y_scale", align_bytes=DMA_ALIGN)
+        y_codes = keep.tile([P, J], U32, name="y_codes", align_bytes=DMA_ALIGN)
+        y_front = keep.tile([P, PACK, 2 * P], F32, name="y_front", tag="raw2", align_bytes=DMA_ALIGN)
+        y_back = keep.tile([P, PACK, 2 * P], F32, name="y_back", align_bytes=DMA_ALIGN)
         y_tiles = [y_front[:, :, :P], y_front[:, :, P:], y_back[:, :, :P], y_back[:, :, P:]]
 
         def product(acc, c, t):

@@ -17,9 +17,10 @@ SILU = mybir.ActivationFunctionType.Silu
 P = 128
 PACK = 4
 QUADS = 4
+SCALE_ROWS = 16
 CHUNKS = J // P
 DMA_ALIGN = 512
-SCALAR_COLS = (0, 128, 128, 0)
+PARK = P - SCALE_ROWS
 
 
 def tile_picked_zdeja_silu_po_kernel(
@@ -33,35 +34,44 @@ def tile_picked_zdeja_silu_po_kernel(
         psum = ctx.enter_context(tc.psum_pool(name="psum", bufs=1))
 
         h_rows = hT.rearrange("(p t) j -> p t j", t=PACK)
-        h_raw = []
 
-        def load_h(c):
-            h_raw.append(keep.tile([P, PACK, P], F32, name="h_raw%d" % c, tag="raw%d" % c, align_bytes=DMA_ALIGN))
-            nc.sync.dma_start(h_raw[c][:], h_rows[:, :, c * P : (c + 1) * P])
-
-        offsets = keep.tile([P, S // 16], U16, name="offsets")
-        table_words = keep.tile([P, T], U32, name="table_words", align_bytes=DMA_ALIGN)
-        words_in = x_words[0].rearrange("p n t -> p (n t)").bitcast(I32)
-        load_h(0)
-        nc.sync.dma_start(offsets[:], offs)
+        def load_h(raw, c):
+            nc.sync.dma_start(raw, h_rows[:, :, c * P : (c + 1) * P])
 
         table_scales = keep.tile([P, T // 4], I32, name="table_scales", align_bytes=DMA_ALIGN)
-        nc.vector.memset(table_scales[:], 0)
-        for q in range(QUADS):
-            queue = nc.scalar if q >= 3 else nc.sync
-            queue.dma_start(
-                table_scales[32 * q : 32 * q + 4, :],
-                x_scales[0, 4 * q : 4 * q + 4, :].bitcast(I32),
-            )
-        nc.sync.dma_start(table_words[:].bitcast(I32), words_in)
+        nc.sync.dma_start(table_scales[PARK:, :], x_scales[0].bitcast(I32))
+        offsets = keep.tile([P, S // 16], U16, name="offsets")
+        nc.sync.dma_start(offsets[:], offs)
+        nc.vector.memset(table_scales[:96, :], 0)
+        nc.vector.memset(table_scales[96:PARK, :], 0)
 
+        h_front = keep.tile([P, last, PACK, P], F32, name="h_front", align_bytes=DMA_ALIGN)
+        load_h(h_front[:, 0], 0)
+        table_words = keep.tile([P, T], U32, name="table_words", align_bytes=DMA_ALIGN)
+        nc.sync.dma_start(table_words[:].bitcast(I32), x_words[0].rearrange("p n t -> p (n t)").bitcast(I32))
+        load_h(h_front[:, 1], 1)
+        load_h(h_front[:, 2], 2)
+
+        x_scale = keep.tile([P, PACK, P // 4], I32, name="x_scale", align_bytes=DMA_ALIGN)
+        nc.vector.memset(x_scale[:], 0)
         warm = keep.tile([P, 8], F32, name="warm")
         warm_out = keep.tile([P, 8], F32, name="warm_out")
         nc.vector.memset(warm[:], 0.0)
         nc.scalar.activation(warm_out[:], warm[:], SILU)
 
-        for c in range(1, CHUNKS):
-            load_h(c)
+        picked = keep.tile([P, S], U8, name="picked", tag="back", align_bytes=DMA_ALIGN)
+        nc.vector.tensor_copy(
+            picked[:].rearrange("p (c t i) -> p c i t", t=PACK, i=4),
+            table_scales[:].bitcast(U8).indirect(offsets[:]),
+        )
+        dealt = keep.tile([P, PACK, P // 4], I32, name="dealt", align_bytes=DMA_ALIGN)
+        nc.vector.tensor_copy(dealt[:], picked[:].bitcast(I32).rearrange("p (c t) -> p t c", t=PACK))
+        for q in range(QUADS):
+            nc.sync.dma_start(x_scale[32 * q : 32 * q + 4], dealt[PARK + 4 * q : PARK + 4 * q + 4])
+
+        h_back = keep.tile([P, PACK, P], F32, name="h_back", tag="back", align_bytes=DMA_ALIGN)
+        load_h(h_back[:], last)
+        h_raw = [h_front[:, c] for c in range(last)] + [h_back[:]]
 
         def interleave(engine_op, grouped, planes):
             engine_op(
@@ -71,13 +81,9 @@ def tile_picked_zdeja_silu_po_kernel(
 
         h_codes, h_scale = {}, {}
 
-        def quantize_h(c):
+        def quantize_h(c, engine_op):
             grouped = keep.tile([P, P, PACK], BF16, name="h_grouped%d" % c, tag="grouped%d" % c, align_bytes=64)
-            cut = SCALAR_COLS[c]
-            if cut:
-                interleave(nc.scalar.copy, grouped[:, :cut, :], h_raw[c][:, :, :cut])
-            if cut < P:
-                interleave(nc.vector.tensor_copy, grouped[:, cut:, :], h_raw[c][:, :, cut:])
+            interleave(engine_op, grouped[:], h_raw[c])
             h_codes[c] = keep.tile([P, P], U32, name="h_codes%d" % c, align_bytes=64)
             h_scale[c] = keep.tile([P, P], U8, name="h_scale%d" % c, align_bytes=64)
             nc.vector.quantize_mx(
@@ -86,29 +92,22 @@ def tile_picked_zdeja_silu_po_kernel(
                 in_=grouped[:].rearrange("p w t -> p (w t)"),
             )
 
-        quantize_h(0)
-        picked = keep.tile([P, S], U8, name="picked", align_bytes=64)
-        nc.vector.tensor_copy(
-            picked[:].rearrange("p (c t i) -> p c i t", t=PACK, i=4),
-            table_scales[:].bitcast(U8).indirect(offsets[:]),
-        )
-        x_scale = keep.tile([P, PACK, P // 4], I32, name="x_scale", align_bytes=64)
-        nc.vector.tensor_copy(x_scale[:], picked[:].bitcast(I32).rearrange("p (c t) -> p t c", t=PACK))
+        quantize_h(0, nc.vector.tensor_copy)
         x_codes = keep.tile([P, S], U32, name="x_codes", align_bytes=64)
         nc.vector.tensor_copy(
             x_codes[:].rearrange("p (t m) -> p m t", t=PACK),
             table_words[:].indirect(offsets[:]),
         )
-        for c in range(1, CHUNKS):
-            quantize_h(c)
+        quantize_h(1, nc.scalar.copy)
+        quantize_h(2, nc.scalar.copy)
+        quantize_h(3, nc.vector.tensor_copy)
 
         y_rows = out_0.rearrange("(p t) j -> p t j", t=PACK)
         words_out = out_1[0].rearrange("p n t -> p (n t)").bitcast(I32)
         y_scale = keep.tile([P, J], U8, name="y_scale", align_bytes=DMA_ALIGN)
         y_codes = keep.tile([P, J], U32, name="y_codes", align_bytes=DMA_ALIGN)
-        y_front = keep.tile([P, PACK, 2 * P], F32, name="y_front", tag="raw2", align_bytes=DMA_ALIGN)
-        y_back = keep.tile([P, PACK, 2 * P], F32, name="y_back", align_bytes=DMA_ALIGN)
-        y_tiles = [y_front[:, :, :P], y_front[:, :, P:], y_back[:, :, :P], y_back[:, :, P:]]
+        y_rest = keep.tile([P, last, PACK, P], F32, name="y_rest", align_bytes=DMA_ALIGN)
+        y_tiles = [h_raw[2]] + [y_rest[:, c] for c in range(last)]
 
         def product(acc, c, t):
             nc.tensor.matmul_mx(
@@ -135,10 +134,8 @@ def tile_picked_zdeja_silu_po_kernel(
                 product(acc[:], c, t)
                 nc.scalar.activation(y_tiles[c][:, t, :], acc[:], SILU)
 
-        def store_y(tiles, cols):
-            source = y_front if cols.start < 2 * P else y_back
-            local = slice(cols.start % (2 * P), cols.start % (2 * P) + cols.stop - cols.start)
-            nc.sync.dma_start(y_rows[:, tiles, cols], source[:, tiles, local])
+        def store_y(c, tiles):
+            nc.sync.dma_start(y_rows[:, tiles, c * P : (c + 1) * P], y_tiles[c][:, tiles, :])
 
         y_grouped = {}
 
@@ -159,16 +156,15 @@ def tile_picked_zdeja_silu_po_kernel(
             )
 
         for c in range(CHUNKS):
-            cols = slice(c * P, (c + 1) * P)
             for half in range(2):
                 if (c, half) == (0, 0):
                     multiply_singly(c)
                 else:
                     multiply(c, half, 2 if (c, half) == (last, 1) else 1)
                 if c < 2:
-                    store_y(slice(2 * half, 2 * half + 2), cols)
+                    store_y(c, slice(2 * half, 2 * half + 2))
             if c >= 2:
-                store_y(slice(0, PACK), cols)
+                store_y(c, slice(0, PACK))
         for c in range(CHUNKS):
             interleave_y(c, 2 if c == last else 1)
             if c:

@@ -20,7 +20,8 @@ QUADS = 4
 SCALE_ROWS = 16
 CHUNKS = J // P
 DMA_ALIGN = 512
-PARK = P - SCALE_ROWS
+PARK = 32
+PORT_ROWS = 4
 
 
 def tile_picked_zdeja_silu_po_kernel(
@@ -31,6 +32,7 @@ def tile_picked_zdeja_silu_po_kernel(
 
     with ExitStack() as ctx:
         keep = ctx.enter_context(tc.tile_pool(name="keep", bufs=1))
+        reuse = ctx.enter_context(tc.tile_pool(name="reuse", bufs=1))
         psum = ctx.enter_context(tc.psum_pool(name="psum", bufs=1))
 
         h_rows = hT.rearrange("(p t) j -> p t j", t=PACK)
@@ -38,15 +40,14 @@ def tile_picked_zdeja_silu_po_kernel(
         def load_h(raw, c):
             nc.sync.dma_start(raw, h_rows[:, :, c * P : (c + 1) * P])
 
-        table_scales = keep.tile([P, T // 4], I32, name="table_scales", align_bytes=DMA_ALIGN)
-        nc.sync.dma_start(table_scales[PARK:, :], x_scales[0].bitcast(I32))
-        offsets = keep.tile([P, S // 16], U16, name="offsets")
-        nc.sync.dma_start(offsets[:], offs)
-        nc.vector.memset(table_scales[:96, :], 0)
-        nc.vector.memset(table_scales[96:PARK, :], 0)
-
+        table_scales = reuse.tile([P, T // 4], I32, name="table_scales", offset=0, align_bytes=DMA_ALIGN)
+        nc.vector.memset(table_scales[:], 0)
         h_front = keep.tile([P, last, PACK, P], F32, name="h_front", align_bytes=DMA_ALIGN)
         load_h(h_front[:, 0], 0)
+        offsets = keep.tile([P, S // 16], U16, name="offsets")
+        nc.sync.dma_start(offsets[:], offs)
+        parked = slice(PARK, PARK + SCALE_ROWS * PORT_ROWS, PORT_ROWS)
+        nc.sync.dma_start(table_scales[parked, :], x_scales[0].bitcast(I32))
         table_words = keep.tile([P, T], U32, name="table_words", align_bytes=DMA_ALIGN)
         nc.sync.dma_start(table_words[:].bitcast(I32), x_words[0].rearrange("p n t -> p (n t)").bitcast(I32))
         load_h(h_front[:, 1], 1)
@@ -59,17 +60,18 @@ def tile_picked_zdeja_silu_po_kernel(
         nc.vector.memset(warm[:], 0.0)
         nc.scalar.activation(warm_out[:], warm[:], SILU)
 
-        picked = keep.tile([P, S], U8, name="picked", tag="back", align_bytes=DMA_ALIGN)
+        picked = keep.tile([P, S], U8, name="picked", align_bytes=DMA_ALIGN)
         nc.vector.tensor_copy(
-            picked[:].rearrange("p (c t i) -> p c i t", t=PACK, i=4),
+            picked[:].rearrange("p (t m) -> p m t", t=PACK),
             table_scales[:].bitcast(U8).indirect(offsets[:]),
         )
-        dealt = keep.tile([P, PACK, P // 4], I32, name="dealt", align_bytes=DMA_ALIGN)
-        nc.vector.tensor_copy(dealt[:], picked[:].bitcast(I32).rearrange("p (c t) -> p t c", t=PACK))
         for q in range(QUADS):
-            nc.sync.dma_start(x_scale[32 * q : 32 * q + 4], dealt[PARK + 4 * q : PARK + 4 * q + 4])
+            nc.sync.dma_start(
+                x_scale[32 * q : 32 * q + 4].rearrange("p t c -> p (t c)"),
+                picked[PARK + 16 * q : PARK + 16 * (q + 1) : PORT_ROWS, :].bitcast(I32),
+            )
 
-        h_back = keep.tile([P, PACK, P], F32, name="h_back", tag="back", align_bytes=DMA_ALIGN)
+        h_back = reuse.tile([P, PACK, P], F32, name="h_back", offset=DMA_ALIGN, align_bytes=DMA_ALIGN)
         load_h(h_back[:], last)
         h_raw = [h_front[:, c] for c in range(last)] + [h_back[:]]
 
@@ -84,7 +86,10 @@ def tile_picked_zdeja_silu_po_kernel(
         def quantize_h(c, engine_op):
             grouped = keep.tile([P, P, PACK], BF16, name="h_grouped%d" % c, tag="grouped%d" % c, align_bytes=64)
             interleave(engine_op, grouped[:], h_raw[c])
-            h_codes[c] = keep.tile([P, P], U32, name="h_codes%d" % c, align_bytes=64)
+            if c == 0:
+                h_codes[c] = reuse.tile([P, P], U32, name="h_codes0", offset=0, align_bytes=DMA_ALIGN)
+            else:
+                h_codes[c] = keep.tile([P, P], U32, name="h_codes%d" % c, align_bytes=64)
             h_scale[c] = keep.tile([P, P], U8, name="h_scale%d" % c, align_bytes=64)
             nc.vector.quantize_mx(
                 out=h_codes[c][:].bitcast(FP8X4),
@@ -92,7 +97,7 @@ def tile_picked_zdeja_silu_po_kernel(
                 in_=grouped[:].rearrange("p w t -> p (w t)"),
             )
 
-        quantize_h(0, nc.vector.tensor_copy)
+        quantize_h(0, nc.scalar.copy)
         x_codes = keep.tile([P, S], U32, name="x_codes", align_bytes=64)
         nc.vector.tensor_copy(
             x_codes[:].rearrange("p (t m) -> p m t", t=PACK),

@@ -20,6 +20,8 @@ QUADS = 4
 SCALE_ROWS = 16
 CHUNKS = J // P
 DMA_ALIGN = 512
+CHUNK_ALIGN = 2048
+TABLE_ALIGN = 4096
 PARK = 32
 PORT_ROWS = 4
 
@@ -40,15 +42,15 @@ def tile_picked_zdeja_silu_po_kernel(
         def load_h(raw, c):
             nc.sync.dma_start(raw, h_rows[:, :, c * P : (c + 1) * P])
 
-        table_scales = reuse.tile([P, T // 4], I32, name="table_scales", offset=0, align_bytes=DMA_ALIGN)
+        table_scales = reuse.tile([P, T // 4], I32, name="table_scales", offset=DMA_ALIGN, align_bytes=DMA_ALIGN)
         nc.vector.memset(table_scales[:], 0)
-        h_front = keep.tile([P, last, PACK, P], F32, name="h_front", align_bytes=DMA_ALIGN)
+        h_front = keep.tile([P, last, PACK, P], F32, name="h_front", align_bytes=CHUNK_ALIGN)
         load_h(h_front[:, 0], 0)
-        offsets = keep.tile([P, S // 16], U16, name="offsets")
+        offsets = keep.tile([P, S // 16], U16, name="offsets", align_bytes=DMA_ALIGN)
         nc.sync.dma_start(offsets[:], offs)
         parked = slice(PARK, PARK + SCALE_ROWS * PORT_ROWS, PORT_ROWS)
         nc.sync.dma_start(table_scales[parked, :], x_scales[0].bitcast(I32))
-        table_words = keep.tile([P, T], U32, name="table_words", align_bytes=DMA_ALIGN)
+        table_words = keep.tile([P, T], U32, name="table_words", align_bytes=TABLE_ALIGN)
         nc.sync.dma_start(table_words[:].bitcast(I32), x_words[0].rearrange("p n t -> p (n t)").bitcast(I32))
         load_h(h_front[:, 1], 1)
         load_h(h_front[:, 2], 2)
@@ -71,7 +73,7 @@ def tile_picked_zdeja_silu_po_kernel(
                 picked[PARK + 16 * q : PARK + 16 * (q + 1) : PORT_ROWS, :].bitcast(I32),
             )
 
-        h_back = reuse.tile([P, PACK, P], F32, name="h_back", offset=DMA_ALIGN, align_bytes=DMA_ALIGN)
+        h_back = reuse.tile([P, PACK, P], F32, name="h_back", offset=CHUNK_ALIGN, align_bytes=CHUNK_ALIGN)
         load_h(h_back[:], last)
         h_raw = [h_front[:, c] for c in range(last)] + [h_back[:]]
 
@@ -87,7 +89,7 @@ def tile_picked_zdeja_silu_po_kernel(
             grouped = keep.tile([P, P, PACK], BF16, name="h_grouped%d" % c, tag="grouped%d" % c, align_bytes=64)
             interleave(engine_op, grouped[:], h_raw[c])
             if c == 0:
-                h_codes[c] = reuse.tile([P, P], U32, name="h_codes0", offset=0, align_bytes=DMA_ALIGN)
+                h_codes[c] = reuse.tile([P, P], U32, name="h_codes0", offset=DMA_ALIGN, align_bytes=DMA_ALIGN)
             else:
                 h_codes[c] = keep.tile([P, P], U32, name="h_codes%d" % c, align_bytes=64)
             h_scale[c] = keep.tile([P, P], U8, name="h_scale%d" % c, align_bytes=64)
@@ -110,8 +112,8 @@ def tile_picked_zdeja_silu_po_kernel(
         y_rows = out_0.rearrange("(p t) j -> p t j", t=PACK)
         words_out = out_1[0].rearrange("p n t -> p (n t)").bitcast(I32)
         y_scale = keep.tile([P, J], U8, name="y_scale", align_bytes=DMA_ALIGN)
-        y_codes = keep.tile([P, J], U32, name="y_codes", align_bytes=DMA_ALIGN)
-        y_rest = keep.tile([P, last, PACK, P], F32, name="y_rest", align_bytes=DMA_ALIGN)
+        y_codes = keep.tile([P, J], U32, name="y_codes", align_bytes=CHUNK_ALIGN)
+        y_rest = keep.tile([P, last, PACK, P], F32, name="y_rest", align_bytes=CHUNK_ALIGN)
         y_tiles = [h_raw[2]] + [y_rest[:, c] for c in range(last)]
 
         def product(acc, c, t):

@@ -154,13 +154,15 @@ def tile_picked_zdeja_silu_po_kernel(
                 cols = slice(part * P // parts, (part + 1) * P // parts)
                 interleave(nc.vector.tensor_copy, y_grouped[c][:, cols, :], y_tiles[c][:, :, cols])
 
-        def quantize_y(c):
-            cols = slice(c * P, (c + 1) * P)
-            nc.vector.quantize_mx(
-                out=y_codes[:, cols].bitcast(FP8X4),
-                scales=y_scale[:, cols],
-                in_=y_grouped[c][:].rearrange("p w t -> p (w t)"),
-            )
+        def quantize_y(c, parts=1):
+            for part in range(parts):
+                local = slice(part * P // parts, (part + 1) * P // parts)
+                cols = slice(c * P + local.start, c * P + local.stop)
+                nc.vector.quantize_mx(
+                    out=y_codes[:, cols].bitcast(FP8X4),
+                    scales=y_scale[:, cols],
+                    in_=y_grouped[c][:, local, :].rearrange("p w t -> p (w t)"),
+                )
 
         for c in range(CHUNKS):
             for half in range(2):
@@ -176,11 +178,11 @@ def tile_picked_zdeja_silu_po_kernel(
             interleave_y(c, 2 if c == last else 1)
             if c:
                 quantize_y(c - 1)
-            if c == 2:
-                nc.sync.dma_start(words_out[:, : J // 2], y_codes[:, : J // 2].bitcast(I32))
-        quantize_y(last)
+            if c == last:
+                nc.sync.dma_start(words_out[:, : last * P], y_codes[:, : last * P].bitcast(I32))
+        quantize_y(last, 2)
 
-        nc.sync.dma_start(words_out[:, J // 2 :], y_codes[:, J // 2 :].bitcast(I32))
+        nc.sync.dma_start(words_out[:, last * P :], y_codes[:, last * P :].bitcast(I32))
         for q in range(QUADS):
             queue = nc.scalar if q == QUADS - 1 else nc.sync
             queue.dma_start(

@@ -85,9 +85,12 @@ def tile_picked_zdeja_silu_po_kernel(
 
         h_codes, h_scale = {}, {}
 
-        def quantize_h(c, engine_op):
+        def quantize_h(c, scalar_tokens):
             grouped = keep.tile([P, P, PACK], BF16, name="h_grouped%d" % c, tag="grouped%d" % c, align_bytes=64)
-            interleave(engine_op, grouped[:], h_raw[c])
+            if scalar_tokens:
+                interleave(nc.scalar.copy, grouped[:, :scalar_tokens, :], h_raw[c][:, :, :scalar_tokens])
+            if scalar_tokens < P:
+                interleave(nc.vector.tensor_copy, grouped[:, scalar_tokens:, :], h_raw[c][:, :, scalar_tokens:])
             if c == 0:
                 h_codes[c] = reuse.tile([P, P], U32, name="h_codes0", offset=DMA_ALIGN, align_bytes=DMA_ALIGN)
             else:
@@ -99,15 +102,15 @@ def tile_picked_zdeja_silu_po_kernel(
                 in_=grouped[:].rearrange("p w t -> p (w t)"),
             )
 
-        quantize_h(0, nc.scalar.copy)
+        quantize_h(0, P)
         x_codes = keep.tile([P, S], U32, name="x_codes", align_bytes=64)
         nc.vector.tensor_copy(
             x_codes[:].rearrange("p (t m) -> p m t", t=PACK),
             table_words[:].indirect(offsets[:]),
         )
-        quantize_h(1, nc.scalar.copy)
-        quantize_h(2, nc.scalar.copy)
-        quantize_h(3, nc.vector.tensor_copy)
+        quantize_h(1, P)
+        quantize_h(2, P // 2)
+        quantize_h(last, 0)
 
         y_rows = out_0.rearrange("(p t) j -> p t j", t=PACK)
         words_out = out_1[0].rearrange("p n t -> p (n t)").bitcast(I32)

from contextlib import ExitStack

import concourse.mybir as mybir

K, T, S, J = 512, 2048, 512, 512
FLOPS = 2 * K * S * J

F32 = mybir.dt.float32
BF16 = mybir.dt.bfloat16
I32 = mybir.dt.int32
U32 = mybir.dt.uint32
U16 = mybir.dt.uint16
U8 = mybir.dt.uint8
FP8X4 = mybir.dt.float8_e4m3fn_x4
SILU = mybir.ActivationFunctionType.Silu

P = 128
PACK = 4
QUADS = 4
SCALE_ROWS = 16
CHUNKS = J // P
DMA_ALIGN = 512
CHUNK_ALIGN = 2048
TABLE_ALIGN = 4096
PARK = 32
PORT_ROWS = 4


def tile_picked_zdeja_silu_po_kernel(
    tc, x_words, x_scales, hT, offs, out_0, out_1, out_2
):
    nc = tc.nc
    last = CHUNKS - 1

    with ExitStack() as ctx:
        keep = ctx.enter_context(tc.tile_pool(name="keep", bufs=1))
        reuse = ctx.enter_context(tc.tile_pool(name="reuse", bufs=1))
        psum = ctx.enter_context(tc.psum_pool(name="psum", bufs=1))

        h_rows = hT.rearrange("(p t) j -> p t j", t=PACK)

        def load_h(raw, c):
            nc.sync.dma_start(raw, h_rows[:, :, c * P : (c + 1) * P])

        table_scales = reuse.tile([P, T // 4], I32, name="table_scales", offset=DMA_ALIGN, align_bytes=DMA_ALIGN)
        nc.vector.memset(table_scales[:], 0)
        h_front = keep.tile([P, last, PACK, P], F32, name="h_front", align_bytes=CHUNK_ALIGN)
        load_h(h_front[:, 0], 0)
        offsets = keep.tile([P, S // 16], U16, name="offsets", align_bytes=DMA_ALIGN)
        nc.sync.dma_start(offsets[:], offs)
        parked = slice(PARK, PARK + SCALE_ROWS * PORT_ROWS, PORT_ROWS)
        nc.sync.dma_start(table_scales[parked, :], x_scales[0].bitcast(I32))
        table_words = keep.tile([P, T], U32, name="table_words", align_bytes=TABLE_ALIGN)
        nc.sync.dma_start(table_words[:].bitcast(I32), x_words[0].rearrange("p n t -> p (n t)").bitcast(I32))
        load_h(h_front[:, 1], 1)
        load_h(h_front[:, 2], 2)

        x_scale = keep.tile([P, PACK, P // 4], I32, name="x_scale", align_bytes=DMA_ALIGN)
        nc.vector.memset(x_scale[:], 0)
        warm = keep.tile([P, 8], F32, name="warm")
        warm_out = keep.tile([P, 8], F32, name="warm_out")
        nc.vector.memset(warm[:], 0.0)
        nc.scalar.activation(warm_out[:], warm[:], SILU)

        picked = keep.tile([P, S], U8, name="picked", align_bytes=DMA_ALIGN)
        nc.vector.tensor_copy(
            picked[:].rearrange("p (t m) -> p m t", t=PACK),
            table_scales[:].bitcast(U8).indirect(offsets[:]),
        )
        for q in range(QUADS):
            nc.sync.dma_start(
                x_scale[32 * q : 32 * q + 4].rearrange("p t c -> p (t c)"),
                picked[PARK + 16 * q : PARK + 16 * (q + 1) : PORT_ROWS, :].bitcast(I32),
            )

        h_back = reuse.tile([P, PACK, P], F32, name="h_back", offset=CHUNK_ALIGN, align_bytes=CHUNK_ALIGN)
        load_h(h_back[:], last)
        h_raw = [h_front[:, c] for c in range(last)] + [h_back[:]]

        def interleave(engine_op, grouped, planes):
            engine_op(
                grouped.rearrange("p (c i) t -> p c t i", i=4),
                planes.rearrange("p t (c i) -> p c t i", i=4),
            )

        h_codes, h_scale = {}, {}

        def quantize_h(c, scalar_tokens):
            grouped = keep.tile([P, P, PACK], BF16, name="h_grouped%d" % c, tag="grouped%d" % c, align_bytes=64)
            if scalar_tokens:
                interleave(nc.scalar.copy, grouped[:, :scalar_tokens, :], h_raw[c][:, :, :scalar_tokens])
            if scalar_tokens < P:
                interleave(nc.vector.tensor_copy, grouped[:, scalar_tokens:, :], h_raw[c][:, :, scalar_tokens:])
            if c == 0:
                h_codes[c] = reuse.tile([P, P], U32, name="h_codes0", offset=DMA_ALIGN, align_bytes=DMA_ALIGN)
            else:
                h_codes[c] = keep.tile([P, P], U32, name="h_codes%d" % c, align_bytes=64)
            h_scale[c] = keep.tile([P, P], U8, name="h_scale%d" % c, align_bytes=64)
            nc.vector.quantize_mx(
                out=h_codes[c][:].bitcast(FP8X4),
                scales=h_scale[c][:],
                in_=grouped[:].rearrange("p w t -> p (w t)"),
            )

        quantize_h(0, P)
        x_codes = keep.tile([P, S], U32, name="x_codes", align_bytes=64)
        nc.vector.tensor_copy(
            x_codes[:].rearrange("p (t m) -> p m t", t=PACK),
            table_words[:].indirect(offsets[:]),
        )
        quantize_h(1, P)
        quantize_h(2, P // 2)
        quantize_h(last, 0)

        y_rows = out_0.rearrange("(p t) j -> p t j", t=PACK)
        words_out = out_1[0].rearrange("p n t -> p (n t)").bitcast(I32)
        y_scale = keep.tile([P, J], U8, name="y_scale", align_bytes=DMA_ALIGN)
        y_codes = keep.tile([P, J], U32, name="y_codes", align_bytes=CHUNK_ALIGN)
        y_rest = keep.tile([P, last, PACK, P], F32, name="y_rest", align_bytes=CHUNK_ALIGN)
        y_tiles = [h_raw[2]] + [y_rest[:, c] for c in range(last)]

        def product(acc, c, t):
            nc.tensor.matmul_mx(
                out=acc,
                lhsT=x_codes[:, t * P : (t + 1) * P].bitcast(FP8X4),
                lhsT_scale=x_scale[:, t, :].bitcast(U8),
                rhs=h_codes[c][:].bitcast(FP8X4),
                rhs_scale=h_scale[c][:],
                start=True,
                stop=True,
            )

        def multiply(c, half, parts=1):
            acc = psum.tile([P, 2, P], F32, name="acc%d_%d" % (c, half), tag="bank%d" % ((2 * c + half) % 7))
            for u in range(2):
                product(acc[:, u, :], c, 2 * half + u)
            for part in range(parts):
                cols = slice(part * P // parts, (part + 1) * P // parts)
                nc.scalar.activation(y_tiles[c][:, 2 * half : 2 * half + 2, cols], acc[:, :, cols], SILU)

        def multiply_singly(c):
            for t in range(2):
                acc = psum.tile([P, P], F32, name="acc_single%d" % t, tag="bank%d" % (7 * t))
                product(acc[:], c, t)
                nc.scalar.activation(y_tiles[c][:, t, :], acc[:], SILU)

        def store_y(c, tiles):
            nc.sync.dma_start(y_rows[:, tiles, c * P : (c + 1) * P], y_tiles[c][:, tiles, :])

        y_grouped = {}

        def interleave_y(c, parts=1):
            y_grouped[c] = keep.tile(
                [P, P, PACK], BF16, name="y_grouped%d" % c, tag="grouped%d" % (last - c), align_bytes=64
            )
            for part in range(parts):
                cols = slice(part * P // parts, (part + 1) * P // parts)
                interleave(nc.vector.tensor_copy, y_grouped[c][:, cols, :], y_tiles[c][:, :, cols])

        def quantize_y(c, parts=1):
            for part in range(parts):
                local = slice(part * P // parts, (part + 1) * P // parts)
                cols = slice(c * P + local.start, c * P + local.stop)
                nc.vector.quantize_mx(
                    out=y_codes[:, cols].bitcast(FP8X4),
                    scales=y_scale[:, cols],
                    in_=y_grouped[c][:, local, :].rearrange("p w t -> p (w t)"),
                )

        for c in range(CHUNKS):
            for half in range(2):
                if (c, half) == (0, 0):
                    multiply_singly(c)
                else:
                    multiply(c, half, 2 if (c, half) == (last, 1) else 1)
                if c < 2:
                    store_y(c, slice(2 * half, 2 * half + 2))
            if c >= 2:
                store_y(c, slice(0, PACK))
        for c in range(CHUNKS):
            interleave_y(c, 2 if c == last else 1)
            if c:
                quantize_y(c - 1)
            if c == last:
                nc.sync.dma_start(words_out[:, : last * P], y_codes[:, : last * P].bitcast(I32))
        quantize_y(last, 2)

        nc.sync.dma_start(words_out[:, last * P :], y_codes[:, last * P :].bitcast(I32))
        for q in range(QUADS):
            queue = nc.scalar if q == QUADS - 1 else nc.sync
            queue.dma_start(
                out_2[0, 4 * q : 4 * q + 4, :].bitcast(I32),
                y_scale[32 * q : 32 * q + 4, :].bitcast(I32),
            )
